import numpy as np
import ml_dtypes


def mxq(x, axis, fmt="e4m3"):
    dtype, down = {"e4m3": (ml_dtypes.float8_e4m3fn, 7), "e5m2": (ml_dtypes.float8_e5m2, 14)}[fmt]
    v = np.moveaxis(np.asarray(x, np.float32).astype(ml_dtypes.bfloat16).astype(np.float64), axis, -1)
    blocks = v.reshape(v.shape[:-1] + (-1, 32))
    amax = np.abs(blocks).max(-1, keepdims=True)
    byte = np.maximum(np.where(amax > 0, np.frexp(amax)[1] - 1 + 127, 0) - down, 1)
    scale = np.exp2(byte - 127.0)
    codes = (blocks / scale).astype(np.float32).astype(dtype).astype(np.float64)
    return np.moveaxis((codes * scale).reshape(v.shape), -1, axis)


WIDE = False


def mx_kscale(k):
    if not WIDE:
        return np.ones(k)
    levels = np.array([10, -10, 5, -5, 0])
    if k % 512:
        return np.exp2(np.random.permutation(np.resize(levels, k // 32))).repeat(32)
    a = np.empty((k // 512, 16))
    for p in range(k // 512):
        a[p, :8] = np.random.permutation(np.resize(levels, 8))
        for g in range(8):
            far = levels[np.abs(levels - a[p, g]) >= 10]
            a[p, g + 8] = far[np.random.randint(len(far))]
    return np.exp2(a.ravel()).repeat(32)


def f64(x):
    return np.asarray(x).astype(np.float64)


def striped(idx):
    return np.tile(idx.reshape(-1, 16).T, (8, 1)).astype(np.uint16)


def unstriped(offs):
    return offs[:16].T.reshape(-1).astype(np.int64)


def pack_weight(w):
    k, n = w.shape
    w = f64(np.asarray(w, np.float32).astype(ml_dtypes.bfloat16)).reshape(k // 32, 32, n)
    amax = np.abs(w).max(1)
    byte = np.clip(np.where(amax > 0, np.frexp(amax)[1] - 1 + 127 - 7, 1), 1, 254)
    scaled = (w * np.exp2(127.0 - byte)[:, None, :]).reshape(k, n).astype(np.float32)
    words = np.ascontiguousarray(scaled.reshape(k // 512, 128, 4, n).transpose(0, 1, 3, 2)).astype(ml_dtypes.float8_e4m3fn).view(np.uint8)
    return words, np.ascontiguousarray(byte.astype(np.uint8).reshape(k // 512, 16, n))


def unpack_weight(words, scales):
    g, p, n, _ = words.shape
    vals = np.ascontiguousarray(words).view(ml_dtypes.float8_e4m3fn).astype(np.float64) * np.repeat(np.exp2(scales.astype(np.float64) - 127.0), 8, axis=1)[..., None]
    return vals.transpose(0, 1, 3, 2).reshape(g * 512, n)


K, T, S, D, N, H, V, U = 1024, 4096, 1024, 4, 256, 512, 256, 512


def setup_inputs():
    n = np.random.standard_normal
    s = mx_kscale(K)[:, None]
    u = mx_kscale(H)
    packed_xT = pack_weight(n((K, T)) * s)
    return {
        "x_words": packed_xT[0],
        "x_scales": packed_xT[1],
        "w1": (n((K, H)) / np.sqrt(K) / s).astype(np.float32),
        "w2": (n((K, H)) / np.sqrt(K) / s).astype(np.float32),
        "sel": (np.random.uniform(0.1, 0.9, (H, U))).astype(np.float32),
        "unit": (np.random.uniform(0.6, 1.4, (H, 1)) * u[:, None]).astype(np.float32),
        "w3": (n((H, N)) / np.sqrt(H) / u[:, None]).astype(np.float32),
        "offs": striped(np.random.permutation(T)[:S]),
        "jn": striped(np.random.permutation(S)),
        "qry": striped(np.random.permutation(np.concatenate([np.arange(V), np.random.randint(0, V, U - V)]))),
    }


def reference(x_words, x_scales, w1, w2, sel, unit, w3, offs, jn, qry):
    xq = unpack_weight(x_words, x_scales)[:, unstriped(offs)]
    cf = mxq(f64(w1), 0, "e4m3").T @ xq
    freq = np.log(np.exp(cf) + 1.0)
    cg = mxq(f64(w2), 0, "e4m3").T @ xq
    frq2 = np.log(np.exp(cg) + 1.0)
    gj = frq2[:, unstriped(jn)]
    match = freq * gj
    size = match.reshape(len(match), -1, D).sum(axis=2)
    sq2 = size[:, unstriped(qry)]
    est = sq2 * f64(sel) + 1.0
    hid = f64(unit) * np.log(est)
    return mxq(f64(w3), 0, "e4m3").T @ mxq(hid, 0, "e4m3")

@@ -1,0 +1,239 @@
+from contextlib import ExitStack
+
+import concourse.mybir as mybir
+
+K, T, S, D, N, H, V, U = 1024, 4096, 1024, 4, 256, 512, 256, 512
+FLOPS = 2 * (2 * K * H * S + H * N * U)
+
+F32 = mybir.dt.float32
+BF16 = mybir.dt.bfloat16
+I32 = mybir.dt.int32
+U32 = mybir.dt.uint32
+U16 = mybir.dt.uint16
+U8 = mybir.dt.uint8
+FP8X4 = mybir.dt.float8_e4m3fn_x4
+ALU = mybir.AluOpType
+ACT = mybir.ActivationFunctionType
+
+P = 128
+PACK = 4
+PASSES = K // (P * PACK)
+BANK = 512
+HALVES = S // BANK
+LIST = 16
+TINY = 2.0 ** -44
+
+
+def tile_picked_yjoinsz_log_p_kernel(tc, x_words, x_scales, w1, w2, sel, unit, w3, offs, jn, qry, out):
+    nc = tc.nc
+    with ExitStack() as ctx:
+        keep = ctx.enter_context(tc.tile_pool(name="keep", bufs=1))
+        psum = ctx.enter_context(tc.psum_pool(name="psum", bufs=1))
+
+        def half(h):
+            return slice(BANK * h, BANK * (h + 1))
+
+        def entries(tile, cols):
+            return tile[:, cols.start // LIST : cols.stop // LIST]
+
+        offs_t = keep.tile([P, S // LIST], U16, name="offs_t")
+        jn_t = keep.tile([P, S // LIST], U16, name="jn_t")
+        qry_t = keep.tile([P, U // LIST], U16, name="qry_t")
+        xw = [keep.tile([P, T], U32, name=f"xw{o}", align_bytes=64) for o in range(PASSES)]
+        xs = keep.tile([P, T], U8, name="xs", align_bytes=64)
+        w_raw = {(a, o): keep.tile([P, PACK, H], F32, name=f"w_raw{a}{o}", align_bytes=64) for a in "gf" for o in range(PASSES)}
+        w3_raw = keep.tile([P, PACK, N], F32, name="w3_raw", align_bytes=64)
+        sel_t = keep.tile([P, PACK, U], F32, name="sel_t", align_bytes=64)
+        unit_t = keep.tile([P, PACK], F32, name="unit_t")
+
+        def load_words(o):
+            nc.sync.dma_start(xw[o][:].bitcast(I32), x_words[o].rearrange("p n t -> p (n t)").bitcast(I32))
+
+        def load_w(a, w, o):
+            nc.sync.dma_start(w_raw[a, o][:], w[512 * o : 512 * (o + 1), :].rearrange("(p j) c -> p j c", j=PACK))
+
+        nc.gpsimd.memset(xs[:].bitcast(I32), 0)
+        load_words(0)
+        nc.sync.dma_start(offs_t[:], offs)
+        for q in range(4):
+            nc.sync.dma_start(xs[32 * q : 32 * q + 4 * PASSES, :].bitcast(I32), x_scales[:, 4 * q : 4 * q + 4, :].bitcast(I32))
+        load_w("g", w2, 0)
+        load_w("g", w2, 1)
+        load_words(1)
+        load_w("f", w1, 0)
+        load_w("f", w1, 1)
+        nc.sync.dma_start(w3_raw[:], w3.rearrange("(p t) n -> p t n", t=PACK))
+        nc.sync.dma_start(jn_t[:], jn)
+        nc.sync.dma_start(qry_t[:], qry)
+        nc.sync.dma_start(unit_t[:], unit.rearrange("(p t) o -> p (t o)", t=PACK))
+        nc.sync.dma_start(sel_t[:], sel.rearrange("(p t) r -> p t r", t=PACK))
+
+        xg = {(o, h): keep.tile([P, BANK], U32, name=f"xg{o}{h}", align_bytes=64) for o in range(PASSES) for h in range(HALVES)}
+        xsg = keep.tile([P, S], U8, name="xsg", align_bytes=64)
+
+        def pick_words(o):
+            for h in range(HALVES):
+                nc.vector.tensor_copy(xg[o, h][:], xw[o][:].indirect(entries(offs_t, half(h))))
+
+        w_codes, w_scales = {}, {}
+
+        def quantise_w(a, o, eng):
+            dealt = keep.tile([P, PACK * H], BF16, name=f"dealt{a}{o}", align_bytes=64)
+            dst = dealt[:].rearrange("p (t m j) -> p m j t", t=PACK, j=PACK)
+            src = w_raw[a, o][:].rearrange("p j (m t) -> p m j t", t=PACK)
+            if eng == "s":
+                nc.scalar.copy(dst, src)
+            elif eng == "g":
+                nc.gpsimd.tensor_scalar(dst, src, 1.0, 0.0, ALU.mult, ALU.add)
+            else:
+                nc.vector.tensor_copy(dst, src)
+            w_codes[a, o] = keep.tile([P, H], U32, name=f"w_codes{a}{o}", align_bytes=64)
+            w_scales[a, o] = keep.tile([P, H], U8, name=f"w_scales{a}{o}", align_bytes=64)
+            nc.vector.quantize_mx(out=w_codes[a, o][:].bitcast(FP8X4), scales=w_scales[a, o][:], in_=dealt[:])
+
+        def product_pass(acc, a, t, h, o):
+            rows = slice(P * t, P * (t + 1))
+            nc.tensor.matmul_mx(
+                out=acc[:],
+                lhsT=w_codes[a, o][:, rows].bitcast(FP8X4),
+                lhsT_scale=w_scales[a, o][:, rows],
+                rhs=xg[o, h][:].bitcast(FP8X4),
+                rhs_scale=xsg[4 * o : P, half(h)],
+                start=(o == 0),
+                stop=(o == PASSES - 1),
+            )
+
+        def banks(a):
+            return {(t, h): psum.tile([P, BANK], F32, name=f"acc{a}{t}{h}", tag=f"bank{HALVES * t + h}") for t in range(PACK) for h in range(HALVES)}
+
+        def log_tiles(a):
+            return [keep.tile([P, S], F32, name=f"log{a}{t}", tag=f"log{t}") for t in range(PACK)]
+
+        def softplus(dst, lg, acc, t):
+            for h in range(HALVES):
+                nc.vector.scalar_tensor_tensor(dst[:, half(h)], lg[t][:, half(h)], -1.0, acc[t, h][:], ALU.mult, ALU.max)
+
+        pick_words(0)
+        nc.vector.tensor_copy(xsg[:], xs[:].indirect(offs_t[:]))
+        quantise_w("g", 0, "s")
+        quantise_w("g", 1, "v")
+        pick_words(1)
+
+        acc, lg = banks("g"), log_tiles("g")
+        order = [(t, h) for h in range(HALVES) for t in range(PACK)]
+        for t, h in order:
+            product_pass(acc[t, h], "g", t, h, 0)
+        for t, h in order:
+            product_pass(acc[t, h], "g", t, h, 1)
+            nc.scalar.activation(lg[t][:, half(h)], acc[t, h][:], ACT.Sigmoid, scale=-1.0)
+
+        quantise_w("f", 0, "v")
+        quantise_w("f", 1, "v")
+        w3_dealt = keep.tile([P, PACK * N], BF16, name="w3_dealt", align_bytes=64)
+        nc.vector.tensor_copy(
+            w3_dealt[:].rearrange("p (c i t) -> p c t i", i=4, t=PACK),
+            w3_raw[:].rearrange("p t (c i) -> p c t i", i=4),
+        )
+        w3_codes = keep.tile([P, N], U32, name="w3_codes", align_bytes=64)
+        w3_scales = keep.tile([P, N], U8, name="w3_scales", align_bytes=64)
+        nc.vector.quantize_mx(out=w3_codes[:].bitcast(FP8X4), scales=w3_scales[:], in_=w3_dealt[:])
+
+        frq2 = [keep.tile([P, S], F32, name=f"frq2{t}") for t in range(PACK)]
+        for t in range(PACK):
+            nc.scalar.activation(lg[t][:], lg[t][:], ACT.Ln, bias=TINY)
+            softplus(frq2[t], lg, acc, t)
+
+        gj = [keep.tile([P, S], F32, name=f"gj{t}") for t in range(PACK)]
+
+        def partners(t, h, on_scalar):
+            window = frq2[t][:].indirect(entries(jn_t, half(h)))
+            if on_scalar:
+                nc.scalar.activation(gj[t][:, half(h)], window, ACT.Copy)
+            else:
+                nc.vector.tensor_copy(gj[t][:, half(h)], window)
+
+        late = ((3, 0), (3, 1))
+        for t in range(PACK):
+            for h in range(HALVES):
+                if (t, h) not in late:
+                    partners(t, h, False)
+
+        acc, lg = banks("f"), log_tiles("f")
+        for t in range(PACK):
+            for h in range(HALVES):
+                for o in range(PASSES):
+                    product_pass(acc[t, h], "f", t, h, o)
+                nc.scalar.activation(lg[t][:, half(h)], acc[t, h][:], ACT.Sigmoid, scale=-1.0)
+        for t in range(PACK):
+            if t == 0:
+                for h in range(HALVES):
+                    nc.scalar.activation(lg[t][:, half(h)], lg[t][:, half(h)], ACT.Ln, bias=TINY)
+            else:
+                nc.scalar.activation(lg[t][:], lg[t][:], ACT.Ln, bias=TINY)
+
+        hid = keep.tile([P, U, PACK], BF16, name="hid", align_bytes=64)
+        planes = keep.tile([P, PACK - 1, U], BF16, name="planes", align_bytes=64)
+        RH = U // 2
+        for t in range(PACK):
+            if t == 2:
+                for lt, lh in late:
+                    partners(lt, lh, True)
+            freq = keep.tile([P, S], F32, name=f"freq{t}", tag="freq", bufs=2)
+            softplus(freq, lg, acc, t)
+            match = keep.tile([P, S], F32, name=f"match{t}", tag="match", bufs=2)
+            joined = keep.tile([P, V + 2 * V], F32, name=f"joined{t}")
+            nc.vector.tensor_tensor(match[:], freq[:], gj[t][:], ALU.mult)
+            m4 = match[:].rearrange("p (v d) -> p v d", d=D)
+            pairs = joined[:, V:].rearrange("p (v d) -> p v d", d=2)
+            nc.vector.tensor_tensor(pairs, m4[:, :, 0:2], m4[:, :, 2:4], ALU.add)
+            nc.vector.tensor_tensor(joined[:, :V], pairs[:, :, 0], pairs[:, :, 1], ALU.add)
+            est = keep.tile([P, U], F32, name=f"est{t}")
+            sq = keep.tile([P, U], F32, name=f"sq{t}")
+            parts = 2 if t == PACK - 1 else 1
+            W = U // parts
+            for c in range(parts):
+                cols = slice(W * c, W * (c + 1))
+                window = joined[:].indirect(entries(qry_t, cols))
+                if t in (0, 1, 2, 3):
+                    nc.scalar.activation(sq[:, cols], window, ACT.Copy)
+                else:
+                    nc.vector.tensor_copy(sq[:, cols], window)
+                (nc.gpsimd if t in () else nc.vector).tensor_tensor(est[:, cols], sq[:, cols], sel_t[:, t, cols], ALU.mult)
+                nc.scalar.activation(est[:, cols], est[:, cols], ACT.Ln, bias=1.0)
+            if t < PACK - 1:
+                if t in (0, 1, 2):
+                    nc.scalar.activation(planes[:, t, :], est[:], ACT.Copy, scale=unit_t[:, t : t + 1])
+                elif t in ():
+                    nc.gpsimd.tensor_scalar(planes[:, t, :], est[:], unit_t[:, t : t + 1], 0.0, ALU.mult, ALU.add)
+                else:
+                    nc.vector.tensor_scalar(planes[:, t, :], est[:], unit_t[:, t : t + 1], None, ALU.mult)
+            if t == PACK - 2:
+                nc.vector.tensor_copy(
+                    hid[:, :, 0 : PACK - 1].rearrange("p (c i) t -> p c t i", i=4),
+                    planes[:].rearrange("p t (c i) -> p c t i", i=4),
+                )
+
+        for c in range(2):
+            cols = slice(RH * c, RH * (c + 1))
+            nc.vector.tensor_scalar(hid[:, cols, PACK - 1], est[:, cols], unit_t[:, PACK - 1 : PACK], None, ALU.mult)
+            hid_codes = keep.tile([P, RH], U32, name=f"hid_codes{c}", align_bytes=64)
+            hid_scales = keep.tile([P, RH], U8, name=f"hid_scales{c}", align_bytes=64)
+            nc.vector.quantize_mx(out=hid_codes[:].bitcast(FP8X4), scales=hid_scales[:], in_=hid[:, cols, :].rearrange("p r t -> p (r t)"))
+            for m in range(N // P):
+                plan = psum.tile([P, BANK], F32, name=f"plan{c}{m}", tag=f"bank{2 * c + m}")
+                rows = slice(P * m, P * (m + 1))
+                nc.tensor.matmul_mx(
+                    out=plan[:, :RH],
+                    lhsT=w3_codes[:, rows].bitcast(FP8X4),
+                    lhsT_scale=w3_scales[:, rows],
+                    rhs=hid_codes[:].bitcast(FP8X4),
+                    rhs_scale=hid_scales[:],
+                    start=True,
+                    stop=True,
+                )
+                res = keep.tile([P, RH], F32, name=f"res{c}{m}")
+                if (c, m) in ((0, 0), (0, 1), (1, 0)):
+                    nc.scalar.copy(res[:], plan[:, :RH])
+                else:
+                    nc.vector.tensor_copy(res[:], plan[:, :RH])
+                nc.sync.dma_start(out[rows, cols], res[:])

@@ -52,11 +52,11 @@ def tile_picked_yjoinsz_log_p_kernel(tc, x_words, x_scales, w1, w2, sel, unit, w
         def load_w(a, w, o):
             nc.sync.dma_start(w_raw[a, o][:], w[512 * o : 512 * (o + 1), :].rearrange("(p j) c -> p j c", j=PACK))
 
-        nc.gpsimd.memset(xs[:].bitcast(I32), 0)
+        nc.vector.memset(xs[:].bitcast(I32), 0)
         load_words(0)
         nc.sync.dma_start(offs_t[:], offs)
         for q in range(4):
-            nc.sync.dma_start(xs[32 * q : 32 * q + 4 * PASSES, :].bitcast(I32), x_scales[:, 4 * q : 4 * q + 4, :].bitcast(I32))
+            nc.gpsimd.dma_start(xs[32 * q : 32 * q + 4 * PASSES, :].bitcast(I32), x_scales[:, 4 * q : 4 * q + 4, :].bitcast(I32))
         load_w("g", w2, 0)
         load_w("g", w2, 1)
         load_words(1)
@@ -69,11 +69,13 @@ def tile_picked_yjoinsz_log_p_kernel(tc, x_words, x_scales, w1, w2, sel, unit, w
         nc.sync.dma_start(sel_t[:], sel.rearrange("(p t) r -> p t r", t=PACK))
 
         xg = {(o, h): keep.tile([P, BANK], U32, name=f"xg{o}{h}", align_bytes=64) for o in range(PASSES) for h in range(HALVES)}
-        xsg = keep.tile([P, S], U8, name="xsg", align_bytes=64)
+        xsg = [keep.tile([P, BANK], U8, name=f"xsg{h}", align_bytes=64) for h in range(HALVES)]
 
-        def pick_words(o):
-            for h in range(HALVES):
-                nc.vector.tensor_copy(xg[o, h][:], xw[o][:].indirect(entries(offs_t, half(h))))
+        def pick_words(o, h):
+            nc.vector.tensor_copy(xg[o, h][:], xw[o][:].indirect(entries(offs_t, half(h))))
+
+        def pick_scales(h):
+            nc.vector.tensor_copy(xsg[h][:], xs[:].indirect(entries(offs_t, half(h))))
 
         w_codes, w_scales = {}, {}
 
@@ -98,7 +100,7 @@ def tile_picked_yjoinsz_log_p_kernel(tc, x_words, x_scales, w1, w2, sel, unit, w
                 lhsT=w_codes[a, o][:, rows].bitcast(FP8X4),
                 lhsT_scale=w_scales[a, o][:, rows],
                 rhs=xg[o, h][:].bitcast(FP8X4),
-                rhs_scale=xsg[4 * o : P, half(h)],
+                rhs_scale=xsg[h][4 * o : P, :],
                 start=(o == 0),
                 stop=(o == PASSES - 1),
             )
@@ -113,11 +115,14 @@ def tile_picked_yjoinsz_log_p_kernel(tc, x_words, x_scales, w1, w2, sel, unit, w
             for h in range(HALVES):
                 nc.vector.scalar_tensor_tensor(dst[:, half(h)], lg[t][:, half(h)], -1.0, acc[t, h][:], ALU.mult, ALU.max)
 
-        pick_words(0)
-        nc.vector.tensor_copy(xsg[:], xs[:].indirect(offs_t[:]))
-        quantise_w("g", 0, "s")
-        quantise_w("g", 1, "v")
-        pick_words(1)
+        pick_words(0, 0)
+        pick_scales(0)
+        quantise_w("g", 0, "v")
+        pick_words(0, 1)
+        pick_scales(1)
+        quantise_w("g", 1, "s")
+        pick_words(1, 0)
+        pick_words(1, 1)
 
         acc, lg = banks("g"), log_tiles("g")
         order = [(t, h) for h in range(HALVES) for t in range(PACK)]
@@ -140,7 +145,11 @@ def tile_picked_yjoinsz_log_p_kernel(tc, x_words, x_scales, w1, w2, sel, unit, w
 
         frq2 = [keep.tile([P, S], F32, name=f"frq2{t}") for t in range(PACK)]
         for t in range(PACK):
-            nc.scalar.activation(lg[t][:], lg[t][:], ACT.Ln, bias=TINY)
+            if t == 0:
+                for h in range(HALVES):
+                    nc.scalar.activation(lg[t][:, half(h)], lg[t][:, half(h)], ACT.Ln, bias=TINY)
+            else:
+                nc.scalar.activation(lg[t][:], lg[t][:], ACT.Ln, bias=TINY)
             softplus(frq2[t], lg, acc, t)
 
         gj = [keep.tile([P, S], F32, name=f"gj{t}") for t in range(PACK)]
@@ -174,44 +183,77 @@ def tile_picked_yjoinsz_log_p_kernel(tc, x_words, x_scales, w1, w2, sel, unit, w
         hid = keep.tile([P, U, PACK], BF16, name="hid", align_bytes=64)
         planes = keep.tile([P, PACK - 1, U], BF16, name="planes", align_bytes=64)
         RH = U // 2
+        freq = [keep.tile([P, S], F32, name=f"freq{t}", tag="freq", bufs=2) for t in range(PACK)]
+        match = [keep.tile([P, S], F32, name=f"match{t}", tag="match", bufs=2) for t in range(PACK)]
+        joined = [keep.tile([P, V + 2 * V], F32, name=f"joined{t}") for t in range(PACK)]
+        sq = [keep.tile([P, U], F32, name=f"sq{t}") for t in range(PACK)]
+        ests = [keep.tile([P, U], F32, name=f"est{t}") for t in range(PACK)]
+
+        def products(t):
+            softplus(freq[t], lg, acc, t)
+            for h in range(HALVES):
+                (nc.gpsimd if (t, h) in () else nc.vector).tensor_tensor(match[t][:, half(h)], freq[t][:, half(h)], gj[t][:, half(h)], ALU.mult)
+
+        def sums(t):
+            if t in ():
+                for h in range(HALVES):
+                    vs = slice(V // HALVES * h, V // HALVES * (h + 1))
+                    nc.vector.tensor_reduce(joined[t][:, vs], match[t][:, half(h)].rearrange("p (v d) -> p v d", d=D), mybir.AxisListType.X, ALU.add)
+                return
+            m4 = match[t][:].rearrange("p (v d) -> p v d", d=D)
+            pairs = joined[t][:, V:].rearrange("p (v d) -> p v d", d=2)
+            for h in range(HALVES):
+                vs = slice(V // HALVES * h, V // HALVES * (h + 1))
+                nc.vector.tensor_tensor(pairs[:, vs, :], m4[:, vs, 0:2], m4[:, vs, 2:4], ALU.add)
+            for h in range(HALVES):
+                vs = slice(V // HALVES * h, V // HALVES * (h + 1))
+                nc.vector.tensor_tensor(joined[t][:, vs], pairs[:, vs, 0], pairs[:, vs, 1], ALU.add)
+
+        def lookup(t, cols):
+            window = joined[t][:].indirect(entries(qry_t, cols))
+            if t in (0, 1, 2, 3):
+                nc.scalar.activation(sq[t][:, cols], window, ACT.Copy)
+            else:
+                nc.vector.tensor_copy(sq[t][:, cols], window)
+
+        def select(t, cols):
+            (nc.gpsimd if t in () else nc.vector).tensor_tensor(ests[t][:, cols], sq[t][:, cols], sel_t[:, t, cols], ALU.mult)
+
+        def logarithm(t, cols):
+            nc.scalar.activation(ests[t][:, cols], ests[t][:, cols], ACT.Ln, bias=1.0)
+
+        def plane(t):
+            if t in (0, 1, 2):
+                nc.scalar.activation(planes[:, t, :], ests[t][:], ACT.Copy, scale=unit_t[:, t : t + 1])
+            elif t in ():
+                nc.gpsimd.tensor_scalar(planes[:, t, :], ests[t][:], unit_t[:, t : t + 1], 0.0, ALU.mult, ALU.add)
+            else:
+                nc.vector.tensor_scalar(planes[:, t, :], ests[t][:], unit_t[:, t : t + 1], None, ALU.mult)
+
+        whole = slice(0, U)
+        last = PACK - 1
         for t in range(PACK):
-            if t == 2:
+            products(t)
+            if t == 1:
                 for lt, lh in late:
                     partners(lt, lh, True)
-            freq = keep.tile([P, S], F32, name=f"freq{t}", tag="freq", bufs=2)
-            softplus(freq, lg, acc, t)
-            match = keep.tile([P, S], F32, name=f"match{t}", tag="match", bufs=2)
-            joined = keep.tile([P, V + 2 * V], F32, name=f"joined{t}")
-            nc.vector.tensor_tensor(match[:], freq[:], gj[t][:], ALU.mult)
-            m4 = match[:].rearrange("p (v d) -> p v d", d=D)
-            pairs = joined[:, V:].rearrange("p (v d) -> p v d", d=2)
-            nc.vector.tensor_tensor(pairs, m4[:, :, 0:2], m4[:, :, 2:4], ALU.add)
-            nc.vector.tensor_tensor(joined[:, :V], pairs[:, :, 0], pairs[:, :, 1], ALU.add)
-            est = keep.tile([P, U], F32, name=f"est{t}")
-            sq = keep.tile([P, U], F32, name=f"sq{t}")
-            parts = 2 if t == PACK - 1 else 1
-            W = U // parts
-            for c in range(parts):
-                cols = slice(W * c, W * (c + 1))
-                window = joined[:].indirect(entries(qry_t, cols))
-                if t in (0, 1, 2, 3):
-                    nc.scalar.activation(sq[:, cols], window, ACT.Copy)
-                else:
-                    nc.vector.tensor_copy(sq[:, cols], window)
-                (nc.gpsimd if t in () else nc.vector).tensor_tensor(est[:, cols], sq[:, cols], sel_t[:, t, cols], ALU.mult)
-                nc.scalar.activation(est[:, cols], est[:, cols], ACT.Ln, bias=1.0)
-            if t < PACK - 1:
-                if t in (0, 1, 2):
-                    nc.scalar.activation(planes[:, t, :], est[:], ACT.Copy, scale=unit_t[:, t : t + 1])
-                elif t in ():
-                    nc.gpsimd.tensor_scalar(planes[:, t, :], est[:], unit_t[:, t : t + 1], 0.0, ALU.mult, ALU.add)
-                else:
-                    nc.vector.tensor_scalar(planes[:, t, :], est[:], unit_t[:, t : t + 1], None, ALU.mult)
-            if t == PACK - 2:
-                nc.vector.tensor_copy(
-                    hid[:, :, 0 : PACK - 1].rearrange("p (c i) t -> p c t i", i=4),
-                    planes[:].rearrange("p t (c i) -> p c t i", i=4),
-                )
+            if t > 0:
+                select(t - 1, whole)
+                logarithm(t - 1, whole)
+                plane(t - 1)
+            sums(t)
+            if t < last:
+                lookup(t, whole)
+        for c in range(2):
+            lookup(last, slice(RH * c, RH * (c + 1)))
+        nc.vector.tensor_copy(
+            hid[:, :, 0 : PACK - 1].rearrange("p (c i) t -> p c t i", i=4),
+            planes[:].rearrange("p t (c i) -> p c t i", i=4),
+        )
+        for c in range(2):
+            select(last, slice(RH * c, RH * (c + 1)))
+            logarithm(last, slice(RH * c, RH * (c + 1)))
+        est = ests[last]
 
         for c in range(2):
             cols = slice(RH * c, RH * (c + 1))

@@ -183,8 +183,8 @@ def tile_picked_yjoinsz_log_p_kernel(tc, x_words, x_scales, w1, w2, sel, unit, w
         hid = keep.tile([P, U, PACK], BF16, name="hid", align_bytes=64)
         planes = keep.tile([P, PACK - 1, U], BF16, name="planes", align_bytes=64)
         RH = U // 2
-        freq = [keep.tile([P, S], F32, name=f"freq{t}", tag="freq", bufs=2) for t in range(PACK)]
-        match = [keep.tile([P, S], F32, name=f"match{t}", tag="match", bufs=2) for t in range(PACK)]
+        freq = lg
+        match = gj
         joined = [keep.tile([P, V + 2 * V], F32, name=f"joined{t}") for t in range(PACK)]
         sq = [keep.tile([P, U], F32, name=f"sq{t}") for t in range(PACK)]
         ests = [keep.tile([P, U], F32, name=f"est{t}") for t in range(PACK)]
@@ -192,10 +192,10 @@ def tile_picked_yjoinsz_log_p_kernel(tc, x_words, x_scales, w1, w2, sel, unit, w
         def products(t):
             softplus(freq[t], lg, acc, t)
             for h in range(HALVES):
-                (nc.gpsimd if (t, h) in () else nc.vector).tensor_tensor(match[t][:, half(h)], freq[t][:, half(h)], gj[t][:, half(h)], ALU.mult)
+                (nc.gpsimd if (t, h) in ((0, 0), (0, 1), (1, 0), (1, 1), (2, 0), (2, 1)) else nc.vector).tensor_tensor(match[t][:, half(h)], freq[t][:, half(h)], gj[t][:, half(h)], ALU.mult)
 
         def sums(t):
-            if t in ():
+            if t in (0, 1, 2):
                 for h in range(HALVES):
                     vs = slice(V // HALVES * h, V // HALVES * (h + 1))
                     nc.vector.tensor_reduce(joined[t][:, vs], match[t][:, half(h)].rearrange("p (v d) -> p v d", d=D), mybir.AxisListType.X, ALU.add)
@@ -217,13 +217,13 @@ def tile_picked_yjoinsz_log_p_kernel(tc, x_words, x_scales, w1, w2, sel, unit, w
                 nc.vector.tensor_copy(sq[t][:, cols], window)
 
         def select(t, cols):
-            (nc.gpsimd if t in () else nc.vector).tensor_tensor(ests[t][:, cols], sq[t][:, cols], sel_t[:, t, cols], ALU.mult)
+            (nc.gpsimd if t in (0, 1) else nc.vector).tensor_tensor(ests[t][:, cols], sq[t][:, cols], sel_t[:, t, cols], ALU.mult)
 
         def logarithm(t, cols):
             nc.scalar.activation(ests[t][:, cols], ests[t][:, cols], ACT.Ln, bias=1.0)
 
         def plane(t):
-            if t in (0, 1, 2):
+            if t in ():
                 nc.scalar.activation(planes[:, t, :], ests[t][:], ACT.Copy, scale=unit_t[:, t : t + 1])
             elif t in ():
                 nc.gpsimd.tensor_scalar(planes[:, t, :], ests[t][:], unit_t[:, t : t + 1], 0.0, ALU.mult, ALU.add)
@@ -232,27 +232,31 @@ def tile_picked_yjoinsz_log_p_kernel(tc, x_words, x_scales, w1, w2, sel, unit, w
 
         whole = slice(0, U)
         last = PACK - 1
-        for t in range(PACK):
-            products(t)
-            if t == 1:
-                for lt, lh in late:
-                    partners(lt, lh, True)
-            if t > 0:
-                select(t - 1, whole)
-                logarithm(t - 1, whole)
-                plane(t - 1)
-            sums(t)
-            if t < last:
-                lookup(t, whole)
+        for lt, lh in late:
+            partners(lt, lh, True)
+        for step in range(PACK + 3):
+            if step < PACK:
+                products(step)
+            t = step - 1
+            if 0 <= t < PACK:
+                sums(t)
+                if t < last:
+                    lookup(t, whole)
+                else:
+                    for c in range(2):
+                        lookup(last, slice(RH * c, RH * (c + 1)))
+            t = step - 3
+            if 0 <= t < last:
+                select(t, whole)
+                logarithm(t, whole)
+                plane(t)
         for c in range(2):
-            lookup(last, slice(RH * c, RH * (c + 1)))
+            select(last, slice(RH * c, RH * (c + 1)))
+            logarithm(last, slice(RH * c, RH * (c + 1)))
         nc.vector.tensor_copy(
             hid[:, :, 0 : PACK - 1].rearrange("p (c i) t -> p c t i", i=4),
             planes[:].rearrange("p t (c i) -> p c t i", i=4),
         )
-        for c in range(2):
-            select(last, slice(RH * c, RH * (c + 1)))
-            logarithm(last, slice(RH * c, RH * (c + 1)))
         est = ests[last]
 
         for c in range(2):
@@ -274,7 +278,7 @@ def tile_picked_yjoinsz_log_p_kernel(tc, x_words, x_scales, w1, w2, sel, unit, w
                     stop=True,
                 )
                 res = keep.tile([P, RH], F32, name=f"res{c}{m}")
-                if (c, m) in ((0, 0), (0, 1), (1, 0)):
+                if (c, m) in ((0, 0), (1, 0)):
                     nc.scalar.copy(res[:], plan[:, :RH])
                 else:
                     nc.vector.tensor_copy(res[:], plan[:, :RH])

from contextlib import ExitStack

import concourse.mybir as mybir

K, T, S, D, N, H, V, U = 1024, 4096, 1024, 4, 256, 512, 256, 512
FLOPS = 2 * (2 * K * H * S + H * N * U)

F32 = mybir.dt.float32
BF16 = mybir.dt.bfloat16
I32 = mybir.dt.int32
U32 = mybir.dt.uint32
U16 = mybir.dt.uint16
U8 = mybir.dt.uint8
FP8X4 = mybir.dt.float8_e4m3fn_x4
ALU = mybir.AluOpType
ACT = mybir.ActivationFunctionType

P = 128
PACK = 4
PASSES = K // (P * PACK)
BANK = 512
HALVES = S // BANK
LIST = 16
TINY = 2.0 ** -44


def tile_picked_yjoinsz_log_p_kernel(tc, x_words, x_scales, w1, w2, sel, unit, w3, offs, jn, qry, out):
    nc = tc.nc
    with ExitStack() as ctx:
        keep = ctx.enter_context(tc.tile_pool(name="keep", bufs=1))
        psum = ctx.enter_context(tc.psum_pool(name="psum", bufs=1))

        def half(h):
            return slice(BANK * h, BANK * (h + 1))

        def entries(tile, cols):
            return tile[:, cols.start // LIST : cols.stop // LIST]

        offs_t = keep.tile([P, S // LIST], U16, name="offs_t")
        jn_t = keep.tile([P, S // LIST], U16, name="jn_t")
        qry_t = keep.tile([P, U // LIST], U16, name="qry_t")
        xw = [keep.tile([P, T], U32, name=f"xw{o}", align_bytes=64) for o in range(PASSES)]
        xs = keep.tile([P, T], U8, name="xs", align_bytes=64)
        w_raw = {(a, o): keep.tile([P, PACK, H], F32, name=f"w_raw{a}{o}", align_bytes=64) for a in "gf" for o in range(PASSES)}
        w3_raw = keep.tile([P, PACK, N], F32, name="w3_raw", align_bytes=64)
        sel_t = keep.tile([P, PACK, U], F32, name="sel_t", align_bytes=64)
        unit_t = keep.tile([P, PACK], F32, name="unit_t")

        def load_words(o):
            nc.sync.dma_start(xw[o][:].bitcast(I32), x_words[o].rearrange("p n t -> p (n t)").bitcast(I32))

        def load_w(a, w, o):
            nc.sync.dma_start(w_raw[a, o][:], w[512 * o : 512 * (o + 1), :].rearrange("(p j) c -> p j c", j=PACK))

        nc.vector.memset(xs[:].bitcast(I32), 0)
        load_words(0)
        nc.sync.dma_start(offs_t[:], offs)
        for q in range(4):
            nc.gpsimd.dma_start(xs[32 * q : 32 * q + 4 * PASSES, :].bitcast(I32), x_scales[:, 4 * q : 4 * q + 4, :].bitcast(I32))
        load_w("g", w2, 0)
        load_w("g", w2, 1)
        load_words(1)
        load_w("f", w1, 0)
        load_w("f", w1, 1)
        nc.sync.dma_start(w3_raw[:], w3.rearrange("(p t) n -> p t n", t=PACK))
        nc.sync.dma_start(jn_t[:], jn)
        nc.sync.dma_start(qry_t[:], qry)
        nc.sync.dma_start(unit_t[:], unit.rearrange("(p t) o -> p (t o)", t=PACK))
        nc.sync.dma_start(sel_t[:], sel.rearrange("(p t) r -> p t r", t=PACK))

        xg = {(o, h): keep.tile([P, BANK], U32, name=f"xg{o}{h}", align_bytes=64) for o in range(PASSES) for h in range(HALVES)}
        xsg = [keep.tile([P, BANK], U8, name=f"xsg{h}", align_bytes=64) for h in range(HALVES)]

        def pick_words(o, h):
            nc.vector.tensor_copy(xg[o, h][:], xw[o][:].indirect(entries(offs_t, half(h))))

        def pick_scales(h):
            nc.vector.tensor_copy(xsg[h][:], xs[:].indirect(entries(offs_t, half(h))))

        w_codes, w_scales = {}, {}

        def quantise_w(a, o, eng):
            dealt = keep.tile([P, PACK * H], BF16, name=f"dealt{a}{o}", align_bytes=64)
            dst = dealt[:].rearrange("p (t m j) -> p m j t", t=PACK, j=PACK)
            src = w_raw[a, o][:].rearrange("p j (m t) -> p m j t", t=PACK)
            if eng == "s":
                nc.scalar.copy(dst, src)
            elif eng == "g":
                nc.gpsimd.tensor_scalar(dst, src, 1.0, 0.0, ALU.mult, ALU.add)
            else:
                nc.vector.tensor_copy(dst, src)
            w_codes[a, o] = keep.tile([P, H], U32, name=f"w_codes{a}{o}", align_bytes=64)
            w_scales[a, o] = keep.tile([P, H], U8, name=f"w_scales{a}{o}", align_bytes=64)
            nc.vector.quantize_mx(out=w_codes[a, o][:].bitcast(FP8X4), scales=w_scales[a, o][:], in_=dealt[:])

        def product_pass(acc, a, t, h, o):
            rows = slice(P * t, P * (t + 1))
            nc.tensor.matmul_mx(
                out=acc[:],
                lhsT=w_codes[a, o][:, rows].bitcast(FP8X4),
                lhsT_scale=w_scales[a, o][:, rows],
                rhs=xg[o, h][:].bitcast(FP8X4),
                rhs_scale=xsg[h][4 * o : P, :],
                start=(o == 0),
                stop=(o == PASSES - 1),
            )

        def banks(a):
            return {(t, h): psum.tile([P, BANK], F32, name=f"acc{a}{t}{h}", tag=f"bank{HALVES * t + h}") for t in range(PACK) for h in range(HALVES)}

        def log_tiles(a):
            return [keep.tile([P, S], F32, name=f"log{a}{t}", tag=f"log{t}") for t in range(PACK)]

        def softplus(dst, lg, acc, t):
            for h in range(HALVES):
                nc.vector.scalar_tensor_tensor(dst[:, half(h)], lg[t][:, half(h)], -1.0, acc[t, h][:], ALU.mult, ALU.max)

        pick_words(0, 0)
        pick_scales(0)
        quantise_w("g", 0, "v")
        pick_words(0, 1)
        pick_scales(1)
        quantise_w("g", 1, "s")
        pick_words(1, 0)
        pick_words(1, 1)

        acc, lg = banks("g"), log_tiles("g")
        order = [(t, h) for h in range(HALVES) for t in range(PACK)]
        for t, h in order:
            product_pass(acc[t, h], "g", t, h, 0)
        for t, h in order:
            product_pass(acc[t, h], "g", t, h, 1)
            nc.scalar.activation(lg[t][:, half(h)], acc[t, h][:], ACT.Sigmoid, scale=-1.0)

        quantise_w("f", 0, "v")
        quantise_w("f", 1, "v")
        w3_dealt = keep.tile([P, PACK * N], BF16, name="w3_dealt", align_bytes=64)
        nc.vector.tensor_copy(
            w3_dealt[:].rearrange("p (c i t) -> p c t i", i=4, t=PACK),
            w3_raw[:].rearrange("p t (c i) -> p c t i", i=4),
        )
        w3_codes = keep.tile([P, N], U32, name="w3_codes", align_bytes=64)
        w3_scales = keep.tile([P, N], U8, name="w3_scales", align_bytes=64)
        nc.vector.quantize_mx(out=w3_codes[:].bitcast(FP8X4), scales=w3_scales[:], in_=w3_dealt[:])

        frq2 = [keep.tile([P, S], F32, name=f"frq2{t}") for t in range(PACK)]
        for t in range(PACK):
            if t == 0:
                for h in range(HALVES):
                    nc.scalar.activation(lg[t][:, half(h)], lg[t][:, half(h)], ACT.Ln, bias=TINY)
            else:
                nc.scalar.activation(lg[t][:], lg[t][:], ACT.Ln, bias=TINY)
            softplus(frq2[t], lg, acc, t)

        gj = [keep.tile([P, S], F32, name=f"gj{t}") for t in range(PACK)]

        def partners(t, h, on_scalar):
            window = frq2[t][:].indirect(entries(jn_t, half(h)))
            if on_scalar:
                nc.scalar.activation(gj[t][:, half(h)], window, ACT.Copy)
            else:
                nc.vector.tensor_copy(gj[t][:, half(h)], window)

        late = ((3, 0), (3, 1))
        for t in range(PACK):
            for h in range(HALVES):
                if (t, h) not in late:
                    partners(t, h, False)

        acc, lg = banks("f"), log_tiles("f")
        for t in range(PACK):
            for h in range(HALVES):
                for o in range(PASSES):
                    product_pass(acc[t, h], "f", t, h, o)
                nc.scalar.activation(lg[t][:, half(h)], acc[t, h][:], ACT.Sigmoid, scale=-1.0)
        for t in range(PACK):
            if t == 0:
                for h in range(HALVES):
                    nc.scalar.activation(lg[t][:, half(h)], lg[t][:, half(h)], ACT.Ln, bias=TINY)
            else:
                nc.scalar.activation(lg[t][:], lg[t][:], ACT.Ln, bias=TINY)

        hid = keep.tile([P, U, PACK], BF16, name="hid", align_bytes=64)
        planes = keep.tile([P, PACK - 1, U], BF16, name="planes", align_bytes=64)
        RH = U // 2
        freq = lg
        match = gj
        joined = [keep.tile([P, V + 2 * V], F32, name=f"joined{t}") for t in range(PACK)]
        sq = [keep.tile([P, U], F32, name=f"sq{t}") for t in range(PACK)]
        ests = [keep.tile([P, U], F32, name=f"est{t}") for t in range(PACK)]

        def products(t):
            softplus(freq[t], lg, acc, t)
            for h in range(HALVES):
                (nc.gpsimd if (t, h) in ((0, 0), (0, 1), (1, 0), (1, 1), (2, 0), (2, 1)) else nc.vector).tensor_tensor(match[t][:, half(h)], freq[t][:, half(h)], gj[t][:, half(h)], ALU.mult)

        def sums(t):
            if t in (0, 1, 2):
                for h in range(HALVES):
                    vs = slice(V // HALVES * h, V // HALVES * (h + 1))
                    nc.vector.tensor_reduce(joined[t][:, vs], match[t][:, half(h)].rearrange("p (v d) -> p v d", d=D), mybir.AxisListType.X, ALU.add)
                return
            m4 = match[t][:].rearrange("p (v d) -> p v d", d=D)
            pairs = joined[t][:, V:].rearrange("p (v d) -> p v d", d=2)
            for h in range(HALVES):
                vs = slice(V // HALVES * h, V // HALVES * (h + 1))
                nc.vector.tensor_tensor(pairs[:, vs, :], m4[:, vs, 0:2], m4[:, vs, 2:4], ALU.add)
            for h in range(HALVES):
                vs = slice(V // HALVES * h, V // HALVES * (h + 1))
                nc.vector.tensor_tensor(joined[t][:, vs], pairs[:, vs, 0], pairs[:, vs, 1], ALU.add)

        def lookup(t, cols):
            window = joined[t][:].indirect(entries(qry_t, cols))
            if t in (0, 1, 2, 3):
                nc.scalar.activation(sq[t][:, cols], window, ACT.Copy)
            else:
                nc.vector.tensor_copy(sq[t][:, cols], window)

        def select(t, cols):
            (nc.gpsimd if t in (0, 1) else nc.vector).tensor_tensor(ests[t][:, cols], sq[t][:, cols], sel_t[:, t, cols], ALU.mult)

        def logarithm(t, cols):
            nc.scalar.activation(ests[t][:, cols], ests[t][:, cols], ACT.Ln, bias=1.0)

        def plane(t):
            if t in ():
                nc.scalar.activation(planes[:, t, :], ests[t][:], ACT.Copy, scale=unit_t[:, t : t + 1])
            elif t in ():
                nc.gpsimd.tensor_scalar(planes[:, t, :], ests[t][:], unit_t[:, t : t + 1], 0.0, ALU.mult, ALU.add)
            else:
                nc.vector.tensor_scalar(planes[:, t, :], ests[t][:], unit_t[:, t : t + 1], None, ALU.mult)

        whole = slice(0, U)
        last = PACK - 1
        for lt, lh in late:
            partners(lt, lh, True)
        for step in range(PACK + 3):
            if step < PACK:
                products(step)
            t = step - 1
            if 0 <= t < PACK:
                sums(t)
                if t < last:
                    lookup(t, whole)
                else:
                    for c in range(2):
                        lookup(last, slice(RH * c, RH * (c + 1)))
            t = step - 3
            if 0 <= t < last:
                select(t, whole)
                logarithm(t, whole)
                plane(t)
        for c in range(2):
            select(last, slice(RH * c, RH * (c + 1)))
            logarithm(last, slice(RH * c, RH * (c + 1)))
        nc.vector.tensor_copy(
            hid[:, :, 0 : PACK - 1].rearrange("p (c i) t -> p c t i", i=4),
            planes[:].rearrange("p t (c i) -> p c t i", i=4),
        )
        est = ests[last]

        for c in range(2):
            cols = slice(RH * c, RH * (c + 1))
            nc.vector.tensor_scalar(hid[:, cols, PACK - 1], est[:, cols], unit_t[:, PACK - 1 : PACK], None, ALU.mult)
            hid_codes = keep.tile([P, RH], U32, name=f"hid_codes{c}", align_bytes=64)
            hid_scales = keep.tile([P, RH], U8, name=f"hid_scales{c}", align_bytes=64)
            nc.vector.quantize_mx(out=hid_codes[:].bitcast(FP8X4), scales=hid_scales[:], in_=hid[:, cols, :].rearrange("p r t -> p (r t)"))
            for m in range(N // P):
                plan = psum.tile([P, BANK], F32, name=f"plan{c}{m}", tag=f"bank{2 * c + m}")
                rows = slice(P * m, P * (m + 1))
                nc.tensor.matmul_mx(
                    out=plan[:, :RH],
                    lhsT=w3_codes[:, rows].bitcast(FP8X4),
                    lhsT_scale=w3_scales[:, rows],
                    rhs=hid_codes[:].bitcast(FP8X4),
                    rhs_scale=hid_scales[:],
                    start=True,
                    stop=True,
                )
                res = keep.tile([P, RH], F32, name=f"res{c}{m}")
                if (c, m) in ((0, 0), (1, 0)):
                    nc.scalar.copy(res[:], plan[:, :RH])
                else:
                    nc.vector.tensor_copy(res[:], plan[:, :RH])
                nc.sync.dma_start(out[rows, cols], res[:])
